import numpy as np
import ml_dtypes


def mxq(x, axis, fmt="e4m3"):
    dtype, down = {"e4m3": (ml_dtypes.float8_e4m3fn, 7), "e5m2": (ml_dtypes.float8_e5m2, 14)}[fmt]
    v = np.moveaxis(np.asarray(x, np.float32).astype(ml_dtypes.bfloat16).astype(np.float64), axis, -1)
    blocks = v.reshape(v.shape[:-1] + (-1, 32))
    amax = np.abs(blocks).max(-1, keepdims=True)
    byte = np.maximum(np.where(amax > 0, np.frexp(amax)[1] - 1 + 127, 0) - down, 1)
    scale = np.exp2(byte - 127.0)
    codes = (blocks / scale).astype(np.float32).astype(dtype).astype(np.float64)
    return np.moveaxis((codes * scale).reshape(v.shape), -1, axis)


WIDE = False


def mx_kscale(k):
    if not WIDE:
        return np.ones(k)
    levels = np.array([10, -10, 5, -5, 0])
    if k % 512:
        return np.exp2(np.random.permutation(np.resize(levels, k // 32))).repeat(32)
    a = np.empty((k // 512, 16))
    for p in range(k // 512):
        a[p, :8] = np.random.permutation(np.resize(levels, 8))
        for g in range(8):
            far = levels[np.abs(levels - a[p, g]) >= 10]
            a[p, g + 8] = far[np.random.randint(len(far))]
    return np.exp2(a.ravel()).repeat(32)


BF16 = ml_dtypes.bfloat16


def bf(x):
    return np.asarray(x, np.float32).astype(BF16)


def f64(x):
    return np.asarray(x).astype(np.float64)


E2M1 = np.array([0.0, 0.5, 1.0, 1.5, 2.0, 3.0, 4.0, 6.0, -0.0, -0.5, -1.0, -1.5, -2.0, -3.0, -4.0, -6.0])


def pack_weight(w, fmt):
    k, n = w.shape
    w = f64(bf(w)).reshape(k // 32, 32, n)
    amax = np.abs(w).max(1)
    if fmt == "e4m3":
        byte = np.frexp(amax)[1] - 1 + 127 - 7
    else:
        mant, ex = np.frexp(amax / 6.0)
        byte = np.where(mant > 0.5, ex, ex - 1) + 127
    byte = np.clip(np.where(amax > 0, byte, 1), 1, 254)
    scaled = (w * np.exp2(127.0 - byte)[:, None, :]).reshape(k, n).astype(np.float32)
    by_word = np.ascontiguousarray(scaled.reshape(k // 512, 128, 4, n).transpose(0, 1, 3, 2))
    if fmt == "e4m3":
        words = by_word.astype(ml_dtypes.float8_e4m3fn).view(np.uint8)
    else:
        c = by_word.astype(ml_dtypes.float4_e2m1fn).view(np.uint8) & 0xF
        words = c[..., 0::2] | (c[..., 1::2] << 4)
    return np.ascontiguousarray(words), np.ascontiguousarray(byte.astype(np.uint8).reshape(k // 512, 16, n))


def unpack_weight(words, scales, fmt):
    g, p, n, _ = words.shape
    if fmt == "e4m3":
        vals = np.ascontiguousarray(words).view(ml_dtypes.float8_e4m3fn).astype(np.float64)
    else:
        nib = np.empty((g, p, n, 4), np.uint8)
        nib[..., 0::2] = words & 0xF
        nib[..., 1::2] = words >> 4
        vals = E2M1[nib]
    vals = vals * np.repeat(np.exp2(scales.astype(np.float64) - 127.0), 8, axis=1)[..., None]
    return vals.transpose(0, 1, 3, 2).reshape(g * 512, n)
def pack4(w):
    words, scales = pack_weight(w, "e2m1")
    return words.reshape(words.shape[0], 128, -1), scales


def unpack4(words, scales):
    return unpack_weight(words.reshape(words.shape[0], 128, -1, 2), scales, "e2m1")


def planes(Y):
    n, m = Y.shape
    b = f64(bf(Y)).reshape(n // 32, 32, m)
    amax = np.abs(b).max(1)
    byte = np.clip(np.where(amax > 0, np.frexp(amax)[1] - 1 + 127 - 7, 1), 1, 254)
    codes = (b * np.exp2(127.0 - byte)[:, None, :]).reshape(n, m).astype(np.float32).astype(ml_dtypes.float8_e4m3fn).view(np.uint8)
    words = codes.reshape(n // 512, 128, 4, m).transpose(0, 1, 3, 2)
    return np.ascontiguousarray(words), np.ascontiguousarray(byte.astype(np.uint8).reshape(n // 512, 16, m))


M, N, KA, KB, F, TOPICS = 1024, 2048, 512, 1024, 512, 16
SHARPNESS, THRESHOLD = 10.0, 0.4

def embed(centres, topic):
    strength = 0.7 + 1.3 * np.random.rand(len(topic), 1)
    e = strength * centres[topic] + np.random.randn(len(topic), KA + KB)
    return e / np.sqrt(np.sum(e * e, axis=1, keepdims=True))

def setup_inputs():
    sa, sb, t = mx_kscale(KA), mx_kscale(KB), mx_kscale(N)
    centres = np.random.randn(TOPICS, KA + KB)
    bank_topic = np.random.randint(0, TOPICS, N)
    batch = SHARPNESS * embed(centres, np.random.randint(0, TOPICS, M))
    bank = embed(centres, bank_topic)
    favour = 0.8 * np.random.randn(TOPICS, F)
    table = np.exp(favour[bank_topic] + 0.5 * np.random.randn(N, F)) * TOPICS / N
    bankb_words, bankb_scales = pack4(bank[:, KA:].T / sb[:, None])
    table_words, table_scales = pack_weight(table / t[:, None], "e4m3")
    return {
        "batch_a": bf(batch[:, :KA] * sa),
        "batch_b": bf(batch[:, KA:] * sb),
        "bank_a": bf(bank[:, :KA] / sa),
        "bankb_words": bankb_words, "bankb_scales": bankb_scales,
        "tau": bf(SHARPNESS * THRESHOLD * (1 + 0.1 * np.random.randn(N))),
        "weight": bf(np.exp(0.4 * np.random.randn(N)) * t),
        "table_words": table_words, "table_scales": table_scales,
        "prior": bf(1 + 0.5 * np.abs(np.random.randn(F))),
        "gain": bf(np.exp(0.8 * np.random.randn(F))),
    }

def reference(batch_a, batch_b, bank_a, bankb_words, bankb_scales, tau, weight, table_words, table_scales, prior, gain):
    za = mxq(f64(batch_a), 1) @ mxq(f64(bank_a), 1).T
    zb = mxq(f64(batch_b), 1) @ unpack4(bankb_words, bankb_scales)
    z = za + zb
    h = f64(weight) / (1 + np.exp(f64(tau) - z))
    d = mxq(h, 1) @ unpack_weight(table_words, table_scales, "e4m3")
    y = f64(gain) * np.log(d + f64(prior))
    Y = y.T
    words, scales = planes(Y)
    return y, words, scales

@@ -1,0 +1,424 @@
+from contextlib import ExitStack
+
+import concourse.mybir as mybir
+from concourse.masks import make_identity
+
+M, N, KA, KB, F = 1024, 2048, 512, 1024, 512
+FLOPS = 2 * M * N * (KA + KB) + 2 * M * N * F
+
+F32 = mybir.dt.float32
+BF16 = mybir.dt.bfloat16
+I32 = mybir.dt.int32
+U8 = mybir.dt.uint8
+FP8X4 = mybir.dt.float8_e4m3fn_x4
+FP4X4 = mybir.dt.float4_e2m1fn_x4
+ACT = mybir.ActivationFunctionType
+ALU = mybir.AluOpType
+
+P = 128
+W = 512
+GROUPS = N // W
+WARMUP = 5
+
+
+def tile_near_duplicate_slice_density_k6_kernel(
+    tc, batch_a, batch_b, bank_a, bankb_words, bankb_scales, tau, weight, table_words, table_scales,
+    prior, gain, out_0, out_1, out_2,
+):
+    nc = tc.nc
+    with ExitStack() as ctx:
+        keep = ctx.enter_context(tc.tile_pool(name="keep", bufs=1))
+        psum = ctx.enter_context(tc.psum_pool(name="psum", bufs=1))
+        ctx.enter_context(tc.manual_schedule())
+
+        def sb(name, shape, dtype, bufs=1, tag=None):
+            return keep.tile(shape, dtype, name=name, tag=tag or name, bufs=bufs, align_bytes=64)
+
+        zbank = [psum.tile([P, W], F32, name=f"zbank{i}") for i in range(4)]
+        tbank = [psum.tile([P, W], F32, name=f"tbank{i}") for i in range(4)]
+
+        src = {}
+        for h in range(2):
+            rows = slice(h * W, (h + 1) * W)
+            src["x", h, 0] = batch_a[rows, :].rearrange("(j p) k -> p j k", p=P)
+            src["x", h, 1] = batch_b[rows, 0:W].rearrange("(j p) k -> p j k", p=P)
+            src["x", h, 2] = batch_b[rows, W:2 * W].rearrange("(j p) k -> p j k", p=P)
+        for g in range(GROUPS):
+            src["bank", g] = bank_a[g * W:(g + 1) * W, :].rearrange("(p j) k -> p j k", j=4)
+        raw, grouped, codes, scales = {}, {}, {}, {}
+
+        def load(u):
+            raw[u] = sb("raw", [P, 4, W], BF16, bufs=7)
+            nc.sync.dma_start(out=raw[u][:], in_=src[u])
+
+        def turn(u, b0):
+            for j in range(4):
+                words = raw[u][:, j, :].bitcast(F32)
+                for e in range(2):
+                    col = ((j % 2) * 2 + e) * P
+                    nc.tensor.transpose(tbank[b0 + j // 2][:, col:col + P], words[:, e:256:2], ident[:])
+
+        def pair_up(u, b0, engines):
+            grouped[u] = sb("grouped", [P, 2, 2 * P * 2], F32, bufs=3)
+            for half in range(2):
+                out = grouped[u][:, half, :].rearrange("p (j r e) -> p j r e", j=2, e=2)
+                in_ = tbank[b0 + half][:].rearrange("p (j e r) -> p j r e", j=2, e=2)
+                if engines[half] == "s":
+                    nc.scalar.copy(out=out, in_=in_)
+                else:
+                    nc.vector.tensor_copy(out=out, in_=in_)
+
+        def quantise(u):
+            codes[u] = sb("codes", [P, W], I32, bufs=10)
+            scales[u] = sb("scales", [P, W], U8, bufs=10)
+            nc.vector.quantize_mx(
+                out=codes[u][:].bitcast(FP8X4), scales=scales[u][:],
+                in_=grouped[u][:].rearrange("p a b -> p (a b)").bitcast(BF16),
+            )
+
+        bw_raw, bw, bs = {}, {}, {}
+
+        def load_bankb_words(g):
+            bw_raw[g] = sb("bw_raw", [P, 2, 2 * W], U8, bufs=4)
+            in_ = bankb_words.rearrange("a p b -> p a b")[:, :, 2 * W * g:2 * W * (g + 1)]
+            nc.sync.dma_start(out=bw_raw[g][:].bitcast(I32), in_=in_.bitcast(I32))
+
+        def load_bankb_scales(queue, tile, c0, c1):
+            for q in range(4):
+                in_ = bankb_scales[:, 4 * q:4 * q + 4, c0:c1].rearrange("a r n -> r a n")
+                queue.dma_start(out=tile[32 * q:32 * q + 4, :, :].bitcast(I32), in_=in_.bitcast(I32))
+
+        def order_bankb_words(g, halves=(0, 1)):
+            if 0 in halves:
+                bw[g] = sb("bw", [P, 2, 2 * W], U8, bufs=4)
+            for a in halves:
+                nc.vector.tensor_copy(
+                    out=bw[g][:, a, :].rearrange("p (t q b) -> p t q b", t=4, b=2),
+                    in_=bw_raw[g][:, a, :].rearrange("p (q t b) -> p t q b", t=4, b=2),
+                )
+
+        def order_bankb_scales(g):
+            bs[g] = sb("bs", [P, 2, W], U8, bufs=4)
+            in_ = bs_first[:] if g == 0 else bs_rest[:, :, (g - 1) * W:g * W]
+            nc.vector.tensor_copy(
+                out=bs[g][:].rearrange("p a (t q) -> p a t q", t=4),
+                in_=in_.rearrange("p a (q t) -> p a t q", t=4),
+            )
+
+        sig, hb, hcodes, hscales = {}, {}, {}, {}
+
+        def gram(h, g, t, a):
+            cols = slice(t * P, (t + 1) * P)
+            if a == 0:
+                lhsT = codes["bank", g][:, cols].bitcast(FP8X4)
+                lhsT_scale = scales["bank", g][:, cols]
+            else:
+                lhsT = bw[g][:, a - 1, 2 * t * P:2 * (t + 1) * P].bitcast(FP4X4)
+                lhsT_scale = bs[g][:, a - 1, cols]
+            nc.tensor.matmul_mx(
+                out=zbank[t][:], lhsT=lhsT, lhsT_scale=lhsT_scale,
+                rhs=codes["x", h, a][:].bitcast(FP8X4), rhs_scale=scales["x", h, a][:],
+                start=(a == 0), stop=(a == 2),
+            )
+
+        def sigmoid(h, g, t):
+            if t == 0:
+                sig[h, g] = sb("sig", [P, 4, W], F32, bufs=4)
+            nc.scalar.activation(
+                out=sig[h, g][:, t, :], in_=zbank[t][:], func=ACT.Sigmoid,
+                bias=neg_tau[:, 4 * g + t:4 * g + t + 1], scale=1.0,
+            )
+
+        def weigh(h, g, part):
+            if part == 0:
+                hb[h, g] = sb("hb", [P, W, 4], BF16, bufs=2)
+            cols = slice(part * 256, (part + 1) * 256)
+            nc.vector.tensor_tensor(
+                out=hb[h, g][:, cols, :].rearrange("p (c i) t -> p c t i", i=2),
+                in0=sig[h, g][:, :, cols].rearrange("p t (c i) -> p c t i", i=2),
+                in1=w2[:, 4 * g:4 * g + 4, :].unsqueeze(1).to_broadcast([P, 128, 4, 2]),
+                op=ALU.mult,
+            )
+
+        def quantise_h(h, g):
+            hcodes[h, g] = sb("hcodes", [P, W], I32, bufs=8)
+            hscales[h, g] = sb("hscales", [P, W], U8, bufs=8)
+            nc.vector.quantize_mx(
+                out=hcodes[h, g][:].bitcast(FP8X4), scales=hscales[h, g][:],
+                in_=hb[h, g][:].rearrange("p m t -> p (m t)"),
+            )
+
+        chunks = [(0, 256), (256, 256), (512, 256), (768, 128), (896, 128)]
+        logd, yt, yb = {}, {}, {}
+
+        ring = tbank + zbank
+        taken = []
+        dbank, ybank = {}, {}
+
+        def next_bank():
+            taken.append(ring[len(taken) % len(ring)])
+            return taken[-1]
+
+        def dplace(c, t):
+            return dbank[c, t][:, 0:chunks[c][1]]
+
+        def totals(c, t):
+            m0, width = chunks[c]
+            h, cols = m0 // W, slice(m0 % W, m0 % W + width)
+            dbank[c, t] = next_bank()
+            for g in range(GROUPS):
+                nc.tensor.matmul_mx(
+                    out=dplace(c, t),
+                    lhsT=tw[:, g, t * P:(t + 1) * P].bitcast(FP8X4), lhsT_scale=ts[4 * g:P, t * P:(t + 1) * P],
+                    rhs=hcodes[h, g][:, cols].bitcast(FP8X4), rhs_scale=hscales[h, g][:, cols],
+                    start=(g == 0), stop=(g == GROUPS - 1),
+                )
+
+        def log_density(c, t):
+            width = chunks[c][1]
+            if t == 0:
+                logd[c] = sb(f"logd{c}", [P, 4, width], F32)
+            nc.scalar.activation(
+                out=logd[c][:, t, :], in_=dplace(c, t), func=ACT.Ln, bias=prior32[:, t:t + 1], scale=1.0,
+            )
+
+        def apply_gain(c, t):
+            width = chunks[c][1]
+            if t == 0:
+                yt[c] = sb(f"yt{c}", [P, 4, width], F32)
+            nc.vector.tensor_scalar(
+                out=yt[c][:, t, :], in0=logd[c][:, t, :], scalar1=gain32[:, t:t + 1], scalar2=None, op0=ALU.mult,
+            )
+
+        def round_y(c):
+            width = chunks[c][1]
+            yb[c] = sb(f"yb{c}", [P, width, 4], BF16)
+            nc.vector.tensor_copy(
+                out=yb[c][:].rearrange("p (c i) t -> p c t i", i=2),
+                in_=yt[c][:].rearrange("p t (c i) -> p c t i", i=2),
+            )
+
+        def quantise_y(c):
+            m0, width = chunks[c]
+            nc.vector.quantize_mx(
+                out=ycodes[:, m0:m0 + width].bitcast(FP8X4), scales=yscales[:, m0:m0 + width],
+                in_=yb[c][:].rearrange("p m t -> p (m t)"),
+            )
+            nc.sync.dma_start(
+                out=out_1[0].rearrange("p m t -> p (m t)").bitcast(I32)[:, m0:m0 + width],
+                in_=ycodes[:, m0:m0 + width],
+            )
+
+        def turn_y(c, j):
+            ybank[c, j] = next_bank()
+            for t in range(4):
+                nc.tensor.transpose(ybank[c, j][:, t * P:(t + 1) * P], yt[c][:, t, j * P:(j + 1) * P], ident[:])
+
+        def store_y(c, j, engine):
+            y = sb("y", [P, F], F32, bufs=6)
+            out = y[:].rearrange("p (q t) -> p q t", t=4)
+            in_ = ybank[c, j][:].rearrange("p (t q) -> p q t", t=4)
+            if engine == "s":
+                nc.scalar.copy(out=out, in_=in_)
+            else:
+                nc.vector.tensor_copy(out=out, in_=in_)
+            m0 = chunks[c][0] + j * P
+            nc.sync.dma_start(out=out_0[m0:m0 + P, :], in_=y[:])
+
+        ident = sb("ident", [P, P], F32)
+        warm = sb("warm", [P, W], BF16)
+        bs_first = sb("bs_first", [P, 2, W], U8)
+        bs_rest = sb("bs_rest", [P, 2, 3 * W], U8)
+        ts_raw = sb("ts_raw", [P, W], U8)
+        ts = sb("ts", [P, W], U8)
+        tw_raw = sb("tw_raw", [P, GROUPS, F], I32)
+        tw = sb("tw", [P, GROUPS, F], I32)
+        tau_raw = sb("tau_raw", [P, GROUPS, 4], BF16)
+        w_raw = sb("w_raw", [P, GROUPS, 4], BF16)
+        prior_raw = sb("prior_raw", [P, 4], BF16)
+        gain_raw = sb("gain_raw", [P, 4], BF16)
+        neg_tau = sb("neg_tau", [P, 4 * GROUPS], F32)
+        w2 = sb("w2", [P, 4 * GROUPS, 2], F32)
+        prior32 = sb("prior32", [P, 4], F32)
+        gain32 = sb("gain32", [P, 4], F32)
+        ycodes = sb("ycodes", [P, M], I32)
+        yscales = sb("yscales", [P, M], U8)
+        first = sb("first", [P, 1], F32)
+
+        x0, x1, x2 = ("x", 0, 0), ("x", 0, 1), ("x", 0, 2)
+        z0, z1, z2 = ("x", 1, 0), ("x", 1, 1), ("x", 1, 2)
+        b0, b1, b2, b3 = (("bank", g) for g in range(GROUPS))
+
+        nc.vector.memset(bs_first[:].rearrange("p a n -> p (a n)").bitcast(I32), 0)
+        nc.vector.memset(warm[:], 0.0)
+        make_identity(nc, ident[:])
+        load(x0)
+        load(b0)
+        load_bankb_scales(nc.scalar, bs_first, 0, W)
+        nc.scalar.activation(out=first[:], in_=warm[:, 0:1], func=ACT.Sigmoid)
+        load(x1)
+        load(x2)
+        load_bankb_words(0)
+        load(b1)
+        nc.vector.memset(bs_rest[:].rearrange("p a n -> p (a n)").bitcast(I32), 0)
+        nc.vector.memset(ts_raw[:].bitcast(I32), 0)
+        nc.sync.dma_start(out=tau_raw[:], in_=tau.rearrange("(g p t) -> p g t", p=P, t=4))
+        nc.sync.dma_start(out=w_raw[:], in_=weight.rearrange("(g p t) -> p g t", p=P, t=4))
+        load_bankb_words(1)
+        load_bankb_scales(nc.sync, bs_rest, W, N)
+        load(b2)
+        load_bankb_words(2)
+        load(b3)
+        load(z0)
+        load_bankb_words(3)
+        load(z1)
+        load(z2)
+        nc.sync.dma_start(out=tw_raw[:], in_=table_words.rearrange("g p f b -> p g (f b)").bitcast(I32))
+        for q in range(4):
+            nc.sync.dma_start(
+                out=ts_raw[32 * q:32 * q + 16, :].bitcast(I32), in_=table_scales[:, 4 * q:4 * q + 4, :].bitcast(I32),
+            )
+        nc.sync.dma_start(out=prior_raw[:], in_=prior.rearrange("(p t) -> p t", t=4))
+        nc.sync.dma_start(out=gain_raw[:], in_=gain.rearrange("(p t) -> p t", t=4))
+        for i in range(WARMUP):
+            nc.tensor.matmul(zbank[0][:], lhsT=warm[:, 0:P], rhs=warm[:], start=True, stop=True)
+
+        def step(h, g):
+            for t in range(4):
+                for a in range(3):
+                    gram(h, g, t, a)
+                sigmoid(h, g, t)
+
+        turn(x0, 0)
+        order_bankb_scales(0)
+        pair_up(x0, 0, "sv")
+        turn(b0, 2)
+        pair_up(b0, 2, "ss")
+        quantise(x0)
+        turn(x1, 0)
+        pair_up(x1, 0, "ss")
+        quantise(b0)
+        turn(x2, 2)
+        pair_up(x2, 2, "ss")
+        quantise(x1)
+        order_bankb_words(0, [0])
+        for t in range(4):
+            gram(0, 0, t, 0)
+        quantise(x2)
+        order_bankb_words(0, [1])
+        nc.vector.tensor_scalar(
+            out=neg_tau[:], in0=tau_raw[:].rearrange("p g t -> p (g t)"), scalar1=-1.0, scalar2=None, op0=ALU.mult,
+        )
+        turn(b1, 0)
+        pair_up(b1, 0, "ss")
+        for t in range(4):
+            gram(0, 0, t, 1)
+            gram(0, 0, t, 2)
+            sigmoid(0, 0, t)
+        order_bankb_words(1)
+        quantise(b1)
+        order_bankb_scales(1)
+        order_bankb_scales(2)
+        order_bankb_scales(3)
+        turn(b2, 2)
+        pair_up(b2, 2, "ss")
+        for i in range(2):
+            nc.vector.tensor_copy(out=w2[:, :, i], in_=w_raw[:].rearrange("p g t -> p (g t)"))
+        order_bankb_words(2)
+        weigh(0, 0, 0)
+        quantise(b2)
+        weigh(0, 0, 1)
+        step(0, 1)
+        turn(b3, 0)
+        pair_up(b3, 0, "ss")
+        turn(z0, 2)
+        pair_up(z0, 2, "ss")
+        order_bankb_words(3)
+        quantise_h(0, 0)
+        weigh(0, 1, 0)
+        quantise(b3)
+        quantise(z0)
+        weigh(0, 1, 1)
+        step(0, 2)
+        turn(z1, 0)
+        pair_up(z1, 0, "ss")
+        turn(z2, 2)
+        pair_up(z2, 2, "ss")
+        nc.vector.tensor_copy(
+            out=tw[:].rearrange("p g (t q) -> p g q t", t=4), in_=tw_raw[:].rearrange("p g (q t) -> p g q t", t=4),
+        )
+        quantise_h(0, 1)
+        nc.vector.tensor_copy(
+            out=ts[:].rearrange("p (t q) -> p t q", t=4), in_=ts_raw[:].rearrange("p (q t) -> p t q", t=4),
+        )
+        weigh(0, 2, 0)
+        quantise(z1)
+        quantise(z2)
+        weigh(0, 2, 1)
+        step(0, 3)
+        nc.vector.tensor_copy(out=prior32[:], in_=prior_raw[:])
+        nc.vector.tensor_copy(out=gain32[:], in_=gain_raw[:])
+        order = [(0, 2), (0, 3), (1, 0), (1, 1), (1, 2), (1, 3)]
+        for i in range(1, 6):
+            if i < 5:
+                step(*order[i + 1])
+            weigh(*order[i], 0)
+            quantise_h(*order[i - 1])
+            weigh(*order[i], 1)
+
+        nc.scalar.activation(out=first[:], in_=prior32[:, 0:1], func=ACT.Ln)
+
+        def slices(c, ts_):
+            for t in ts_:
+                totals(c, t)
+                log_density(c, t)
+
+        def gains(c, ts_):
+            for t in ts_:
+                apply_gain(c, t)
+
+        slices(0, range(4))
+        slices(1, range(4))
+        gains(0, [0])
+        quantise_h(1, 3)
+        gains(0, [1, 2, 3])
+        slices(2, [0, 1])
+        gains(1, range(4))
+        round_y(0)
+        for j in range(2):
+            turn_y(0, j)
+        store_y(0, 0, "s")
+        gains(2, [0])
+        quantise_y(0)
+        store_y(0, 1, "v")
+        slices(2, [2, 3])
+        for j in range(2):
+            turn_y(1, j)
+            store_y(1, j, "s")
+        round_y(1)
+        gains(2, [1, 2, 3])
+        quantise_y(1)
+        slices(3, range(4))
+        round_y(2)
+        gains(3, [0, 1])
+        quantise_y(2)
+        gains(3, [2, 3])
+        for j in range(2):
+            turn_y(2, j)
+        store_y(2, 0, "s")
+        store_y(2, 1, "v")
+        slices(4, range(4))
+        round_y(3)
+        gains(4, [0, 1])
+        quantise_y(3)
+        gains(4, [2, 3])
+        turn_y(3, 0)
+        store_y(3, 0, "s")
+        turn_y(4, 0)
+        round_y(4)
+        quantise_y(4)
+        for q in range(4):
+            nc.sync.dma_start(
+                out=out_2[0, 4 * q:4 * q + 4, :].bitcast(I32), in_=yscales[32 * q:32 * q + 4, :].bitcast(I32),
+            )
+        store_y(4, 0, "s")

@@ -18,7 +18,7 @@ ALU = mybir.AluOpType
 P = 128
 W = 512
 GROUPS = N // W
-WARMUP = 5
+WARMUP = 4
 
 
 def tile_near_duplicate_slice_density_k6_kernel(
@@ -45,18 +45,28 @@ def tile_near_duplicate_slice_density_k6_kernel(
             src["x", h, 2] = batch_b[rows, W:2 * W].rearrange("(j p) k -> p j k", p=P)
         for g in range(GROUPS):
             src["bank", g] = bank_a[g * W:(g + 1) * W, :].rearrange("(p j) k -> p j k", j=4)
-        raw, grouped, codes, scales = {}, {}, {}, {}
+        raw, split, grouped, codes, scales = {}, {}, {}, {}, {}
 
-        def load(u):
+        def load(u, pieces=1):
             raw[u] = sb("raw", [P, 4, W], BF16, bufs=7)
-            nc.sync.dma_start(out=raw[u][:], in_=src[u])
+            for i in range(pieces):
+                js = slice(i * 4 // pieces, (i + 1) * 4 // pieces)
+                nc.sync.dma_start(out=raw[u][:, js, :], in_=src[u][:, js, :])
+
+        def split_words(u):
+            split[u] = sb("split", [P, 4, 2, P], F32, bufs=2)
+            nc.vector.tensor_copy(
+                out=split[u][:].rearrange("p j e q -> p j q e"),
+                in_=raw[u][:].rearrange("p j k -> p (j k)").bitcast(F32).rearrange("p (j q e) -> p j q e", j=4, e=2),
+            )
 
         def turn(u, b0):
             for j in range(4):
                 words = raw[u][:, j, :].bitcast(F32)
                 for e in range(2):
                     col = ((j % 2) * 2 + e) * P
-                    nc.tensor.transpose(tbank[b0 + j // 2][:, col:col + P], words[:, e:256:2], ident[:])
+                    in_ = split[u][:, j, e, :] if u in split else words[:, e:256:2]
+                    nc.tensor.transpose(tbank[b0 + j // 2][:, col:col + P], in_, ident[:])
 
         def pair_up(u, b0, engines):
             grouped[u] = sb("grouped", [P, 2, 2 * P * 2], F32, bufs=3)
@@ -76,17 +86,12 @@ def tile_near_duplicate_slice_density_k6_kernel(
                 in_=grouped[u][:].rearrange("p a b -> p (a b)").bitcast(BF16),
             )
 
-        bw_raw, bw, bs = {}, {}, {}
+        bw_raw, bw = {}, {}
 
         def load_bankb_words(g):
             bw_raw[g] = sb("bw_raw", [P, 2, 2 * W], U8, bufs=4)
             in_ = bankb_words.rearrange("a p b -> p a b")[:, :, 2 * W * g:2 * W * (g + 1)]
             nc.sync.dma_start(out=bw_raw[g][:].bitcast(I32), in_=in_.bitcast(I32))
-
-        def load_bankb_scales(queue, tile, c0, c1):
-            for q in range(4):
-                in_ = bankb_scales[:, 4 * q:4 * q + 4, c0:c1].rearrange("a r n -> r a n")
-                queue.dma_start(out=tile[32 * q:32 * q + 4, :, :].bitcast(I32), in_=in_.bitcast(I32))
 
         def order_bankb_words(g, halves=(0, 1)):
             if 0 in halves:
@@ -97,14 +102,6 @@ def tile_near_duplicate_slice_density_k6_kernel(
                     in_=bw_raw[g][:, a, :].rearrange("p (q t b) -> p t q b", t=4, b=2),
                 )
 
-        def order_bankb_scales(g):
-            bs[g] = sb("bs", [P, 2, W], U8, bufs=4)
-            in_ = bs_first[:] if g == 0 else bs_rest[:, :, (g - 1) * W:g * W]
-            nc.vector.tensor_copy(
-                out=bs[g][:].rearrange("p a (t q) -> p a t q", t=4),
-                in_=in_.rearrange("p a (q t) -> p a t q", t=4),
-            )
-
         sig, hb, hcodes, hscales = {}, {}, {}, {}
 
         def gram(h, g, t, a):
@@ -114,7 +111,7 @@ def tile_near_duplicate_slice_density_k6_kernel(
                 lhsT_scale = scales["bank", g][:, cols]
             else:
                 lhsT = bw[g][:, a - 1, 2 * t * P:2 * (t + 1) * P].bitcast(FP4X4)
-                lhsT_scale = bs[g][:, a - 1, cols]
+                lhsT_scale = bs[:, g, a - 1, cols]
             nc.tensor.matmul_mx(
                 out=zbank[t][:], lhsT=lhsT, lhsT_scale=lhsT_scale,
                 rhs=codes["x", h, a][:].bitcast(FP8X4), rhs_scale=scales["x", h, a][:],
@@ -227,8 +224,9 @@ def tile_near_duplicate_slice_density_k6_kernel(
 
         ident = sb("ident", [P, P], F32)
         warm = sb("warm", [P, W], BF16)
-        bs_first = sb("bs_first", [P, 2, W], U8)
-        bs_rest = sb("bs_rest", [P, 2, 3 * W], U8)
+        bs_raw = sb("bs_raw", [P, W], U8)
+        bs_ordered = sb("bs_ordered", [P, W], U8)
+        bs = sb("bs", [P, GROUPS, 2, W], U8)
         ts_raw = sb("ts_raw", [P, W], U8)
         ts = sb("ts", [P, W], U8)
         tw_raw = sb("tw_raw", [P, GROUPS, F], I32)
@@ -249,24 +247,34 @@ def tile_near_duplicate_slice_density_k6_kernel(
         z0, z1, z2 = ("x", 1, 0), ("x", 1, 1), ("x", 1, 2)
         b0, b1, b2, b3 = (("bank", g) for g in range(GROUPS))
 
-        nc.vector.memset(bs_first[:].rearrange("p a n -> p (a n)").bitcast(I32), 0)
-        nc.vector.memset(warm[:], 0.0)
+        nc.gpsimd.memset(warm[:], 0.0)
         make_identity(nc, ident[:])
-        load(x0)
-        load(b0)
-        load_bankb_scales(nc.scalar, bs_first, 0, W)
+        load(x0, 2)
+        for a in range(2):
+            nc.scalar.dma_start(
+                out=bs_raw[a:P:2, :].bitcast(I32),
+                in_=bankb_scales[a].rearrange("q (g n) -> (q g) n", g=GROUPS).bitcast(I32),
+            )
         nc.scalar.activation(out=first[:], in_=warm[:, 0:1], func=ACT.Sigmoid)
-        load(x1)
-        load(x2)
+        load(b0, 2)
+        load(x1, 2)
+        load(x2, 2)
         load_bankb_words(0)
-        load(b1)
-        nc.vector.memset(bs_rest[:].rearrange("p a n -> p (a n)").bitcast(I32), 0)
+        nc.vector.memset(bs[:].rearrange("p g a n -> p (g a n)").bitcast(I32), 0)
         nc.vector.memset(ts_raw[:].bitcast(I32), 0)
+        nc.vector.tensor_copy(
+            out=bs_ordered[:].rearrange("p (t q) -> p t q", t=4), in_=bs_raw[:].rearrange("p (q t) -> p t q", t=4),
+        )
+        load(b1)
+        for q in (0, 2, 1, 3):
+            nc.sync.dma_start(
+                out=bs[32 * q:32 * q + 4].rearrange("p g a n -> p (g a) n").bitcast(I32),
+                in_=bs_ordered[32 * q:32 * (q + 1), :].bitcast(I32),
+            )
         nc.sync.dma_start(out=tau_raw[:], in_=tau.rearrange("(g p t) -> p g t", p=P, t=4))
-        nc.sync.dma_start(out=w_raw[:], in_=weight.rearrange("(g p t) -> p g t", p=P, t=4))
         load_bankb_words(1)
-        load_bankb_scales(nc.sync, bs_rest, W, N)
         load(b2)
+        nc.sync.dma_start(out=w_raw[:], in_=weight.rearrange("(g p t) -> p g t", p=P, t=4))
         load_bankb_words(2)
         load(b3)
         load(z0)
@@ -280,8 +288,12 @@ def tile_near_duplicate_slice_density_k6_kernel(
             )
         nc.sync.dma_start(out=prior_raw[:], in_=prior.rearrange("(p t) -> p t", t=4))
         nc.sync.dma_start(out=gain_raw[:], in_=gain.rearrange("(p t) -> p t", t=4))
+
+        def keep_warm(width):
+            nc.tensor.matmul(zbank[0][:, 0:width], lhsT=warm[:, 0:P], rhs=warm[:, 0:width], start=True, stop=True)
+
         for i in range(WARMUP):
-            nc.tensor.matmul(zbank[0][:], lhsT=warm[:, 0:P], rhs=warm[:], start=True, stop=True)
+            keep_warm(W)
 
         def step(h, g):
             for t in range(4):
@@ -290,14 +302,16 @@ def tile_near_duplicate_slice_density_k6_kernel(
                 sigmoid(h, g, t)
 
         turn(x0, 0)
-        order_bankb_scales(0)
         pair_up(x0, 0, "sv")
+        keep_warm(256)
         turn(b0, 2)
         pair_up(b0, 2, "ss")
         quantise(x0)
+        keep_warm(256)
         turn(x1, 0)
         pair_up(x1, 0, "ss")
         quantise(b0)
+        keep_warm(256)
         turn(x2, 2)
         pair_up(x2, 2, "ss")
         quantise(x1)
@@ -317,9 +331,6 @@ def tile_near_duplicate_slice_density_k6_kernel(
             sigmoid(0, 0, t)
         order_bankb_words(1)
         quantise(b1)
-        order_bankb_scales(1)
-        order_bankb_scales(2)
-        order_bankb_scales(3)
         turn(b2, 2)
         pair_up(b2, 2, "ss")
         for i in range(2):

@@ -31,89 +31,97 @@ def tile_near_duplicate_slice_density_k6_kernel(
         psum = ctx.enter_context(tc.psum_pool(name="psum", bufs=1))
         ctx.enter_context(tc.manual_schedule())
 
-        def sb(name, shape, dtype, bufs=1, tag=None):
-            return keep.tile(shape, dtype, name=name, tag=tag or name, bufs=bufs, align_bytes=64)
+        def sb(name, shape, dtype, bufs=1):
+            return keep.tile(shape, dtype, name=name, tag=name, bufs=bufs, align_bytes=64)
 
-        zbank = [psum.tile([P, W], F32, name=f"zbank{i}") for i in range(4)]
-        tbank = [psum.tile([P, W], F32, name=f"tbank{i}") for i in range(4)]
+        ring = [psum.tile([P, W], F32, name=f"bank{i}") for i in range(8)]
+        taken = []
 
-        src = {}
-        for h in range(2):
-            rows = slice(h * W, (h + 1) * W)
-            src["x", h, 0] = batch_a[rows, :].rearrange("(j p) k -> p j k", p=P)
-            src["x", h, 1] = batch_b[rows, 0:W].rearrange("(j p) k -> p j k", p=P)
-            src["x", h, 2] = batch_b[rows, W:2 * W].rearrange("(j p) k -> p j k", p=P)
-        for g in range(GROUPS):
-            src["bank", g] = bank_a[g * W:(g + 1) * W, :].rearrange("(p j) k -> p j k", j=4)
-        raw, split, grouped, codes, scales = {}, {}, {}, {}, {}
+        def next_bank():
+            taken.append(ring[len(taken) % len(ring)])
+            return taken[-1]
 
-        def load(u, pieces=1):
-            raw[u] = sb("raw", [P, 4, W], BF16, bufs=7)
-            for i in range(pieces):
-                js = slice(i * 4 // pieces, (i + 1) * 4 // pieces)
-                nc.sync.dma_start(out=raw[u][:, js, :], in_=src[u][:, js, :])
+        raw, split, grouped, codes, scales, turned = {}, {}, {}, {}, {}, {}
+
+        def load(name, i, pieces=1):
+            source = {"xa": batch_a, "xb": batch_b, "bank": bank_a}[name]
+            k = source.shape[1]
+            tile = sb("raw_wide", [P, 4, k], BF16, bufs=2) if name == "xb" else sb("raw", [P, 4, k], BF16, bufs=4)
+            rows = source[i * W:(i + 1) * W, :].rearrange("(p j) k -> p j k", j=4)
+            for piece in range(pieces):
+                js = slice(piece * 4 // pieces, (piece + 1) * 4 // pieces)
+                nc.sync.dma_start(out=tile[:, js, :], in_=rows[:, js, :])
+            if name == "xb":
+                raw["x", i, 1], raw["x", i, 2] = tile[:, :, 0:W], tile[:, :, W:2 * W]
+            elif name == "xa":
+                raw["x", i, 0] = tile[:]
+            else:
+                raw["bank", i] = tile[:]
 
         def split_words(u):
-            split[u] = sb("split", [P, 4, 2, P], F32, bufs=2)
+            split[u] = sb("split", [P, 4, 2, P], F32, bufs=4)
             nc.vector.tensor_copy(
                 out=split[u][:].rearrange("p j e q -> p j q e"),
-                in_=raw[u][:].rearrange("p j k -> p (j k)").bitcast(F32).rearrange("p (j q e) -> p j q e", j=4, e=2),
+                in_=raw[u].bitcast(F32).rearrange("p j (q e) -> p j q e", e=2),
             )
 
-        def turn(u, b0):
-            for j in range(4):
-                words = raw[u][:, j, :].bitcast(F32)
+        def turn(u, half, jjs=(0, 1)):
+            if 0 in jjs:
+                turned[u, half] = next_bank()
+            for jj in jjs:
+                j = 2 * half + jj
                 for e in range(2):
-                    col = ((j % 2) * 2 + e) * P
-                    in_ = split[u][:, j, e, :] if u in split else words[:, e:256:2]
-                    nc.tensor.transpose(tbank[b0 + j // 2][:, col:col + P], in_, ident[:])
+                    in_ = split[u][:, j, e, :] if u in split else raw[u][:, j, :].bitcast(F32)[:, e:256:2]
+                    col = (2 * jj + e) * P
+                    nc.tensor.transpose(turned[u, half][:, col:col + P], in_, ident[:])
 
-        def pair_up(u, b0, engines):
-            grouped[u] = sb("grouped", [P, 2, 2 * P * 2], F32, bufs=3)
-            for half in range(2):
-                out = grouped[u][:, half, :].rearrange("p (j r e) -> p j r e", j=2, e=2)
-                in_ = tbank[b0 + half][:].rearrange("p (j e r) -> p j r e", j=2, e=2)
-                if engines[half] == "s":
-                    nc.scalar.copy(out=out, in_=in_)
-                else:
-                    nc.vector.tensor_copy(out=out, in_=in_)
+        def pair_up(u, half, engine="s"):
+            if half == 0:
+                grouped[u] = sb("grouped", [P, 2 * W], F32, bufs=4)
+            if u[0] == "bank":
+                out = grouped[u][:].rearrange("p (h j r e) -> p h j r e", h=2, j=2, e=2)[:, half]
+                in_ = turned[u, half][:].rearrange("p (j e r) -> p j r e", j=2, e=2)
+            else:
+                out = grouped[u][:].rearrange("p (r h j e) -> p h r j e", h=2, j=2, e=2)[:, half]
+                in_ = turned[u, half][:].rearrange("p (j e r) -> p r j e", j=2, e=2)
+            if engine == "s":
+                nc.scalar.copy(out=out, in_=in_)
+            else:
+                nc.vector.tensor_copy(out=out, in_=in_)
 
         def quantise(u):
             codes[u] = sb("codes", [P, W], I32, bufs=10)
             scales[u] = sb("scales", [P, W], U8, bufs=10)
-            nc.vector.quantize_mx(
-                out=codes[u][:].bitcast(FP8X4), scales=scales[u][:],
-                in_=grouped[u][:].rearrange("p a b -> p (a b)").bitcast(BF16),
-            )
+            nc.vector.quantize_mx(out=codes[u][:].bitcast(FP8X4), scales=scales[u][:], in_=grouped[u][:].bitcast(BF16))
 
         bw_raw, bw = {}, {}
 
-        def load_bankb_words(g):
-            bw_raw[g] = sb("bw_raw", [P, 2, 2 * W], U8, bufs=4)
-            in_ = bankb_words.rearrange("a p b -> p a b")[:, :, 2 * W * g:2 * W * (g + 1)]
-            nc.sync.dma_start(out=bw_raw[g][:].bitcast(I32), in_=in_.bitcast(I32))
+        def load_bankb_words(a, pair):
+            tile = sb("bw_raw", [P, 2, 2 * W], U8, bufs=4)
+            in_ = bankb_words[a, :, 4 * W * pair:4 * W * (pair + 1)]
+            nc.sync.dma_start(out=tile[:].rearrange("p g b -> p (g b)").bitcast(I32), in_=in_.bitcast(I32))
+            bw_raw[2 * pair, a], bw_raw[2 * pair + 1, a] = tile[:, 0, :], tile[:, 1, :]
 
-        def order_bankb_words(g, halves=(0, 1)):
-            if 0 in halves:
-                bw[g] = sb("bw", [P, 2, 2 * W], U8, bufs=4)
-            for a in halves:
-                nc.vector.tensor_copy(
-                    out=bw[g][:, a, :].rearrange("p (t q b) -> p t q b", t=4, b=2),
-                    in_=bw_raw[g][:, a, :].rearrange("p (q t b) -> p t q b", t=4, b=2),
-                )
+        def order_bankb_words(g, a):
+            bw[g, a] = sb("bw", [P, 2 * W], U8, bufs=8)
+            nc.vector.tensor_copy(
+                out=bw[g, a][:].rearrange("p (t q b) -> p t q b", t=4, b=2),
+                in_=bw_raw[g, a].rearrange("p (q t b) -> p t q b", t=4, b=2),
+            )
 
-        sig, hb, hcodes, hscales = {}, {}, {}, {}
+        zbank, sig, hb, hcodes, hscales = {}, {}, {}, {}, {}
 
         def gram(h, g, t, a):
             cols = slice(t * P, (t + 1) * P)
             if a == 0:
+                zbank[h, g, t] = next_bank()
                 lhsT = codes["bank", g][:, cols].bitcast(FP8X4)
                 lhsT_scale = scales["bank", g][:, cols]
             else:
-                lhsT = bw[g][:, a - 1, 2 * t * P:2 * (t + 1) * P].bitcast(FP4X4)
+                lhsT = bw[g, a - 1][:, 2 * t * P:2 * (t + 1) * P].bitcast(FP4X4)
                 lhsT_scale = bs[:, g, a - 1, cols]
             nc.tensor.matmul_mx(
-                out=zbank[t][:], lhsT=lhsT, lhsT_scale=lhsT_scale,
+                out=zbank[h, g, t][:], lhsT=lhsT, lhsT_scale=lhsT_scale,
                 rhs=codes["x", h, a][:].bitcast(FP8X4), rhs_scale=scales["x", h, a][:],
                 start=(a == 0), stop=(a == 2),
             )
@@ -122,7 +130,7 @@ def tile_near_duplicate_slice_density_k6_kernel(
             if t == 0:
                 sig[h, g] = sb("sig", [P, 4, W], F32, bufs=4)
             nc.scalar.activation(
-                out=sig[h, g][:, t, :], in_=zbank[t][:], func=ACT.Sigmoid,
+                out=sig[h, g][:, t, :], in_=zbank[h, g, t][:], func=ACT.Sigmoid,
                 bias=neg_tau[:, 4 * g + t:4 * g + t + 1], scale=1.0,
             )
 
@@ -137,35 +145,42 @@ def tile_near_duplicate_slice_density_k6_kernel(
                 op=ALU.mult,
             )
 
-        def quantise_h(h, g):
-            hcodes[h, g] = sb("hcodes", [P, W], I32, bufs=8)
-            hscales[h, g] = sb("hscales", [P, W], U8, bufs=8)
+        hrows = {}
+
+        def weigh_rows(h, g, t):
+            if t == 0:
+                hrows[h, g] = sb("hrows", [P, 4, W], BF16, bufs=1)
+            nc.scalar.activation(
+                out=hrows[h, g][:, t, :], in_=sig[h, g][:, t, :], func=ACT.Copy, scale=w2[:, 4 * g + t, 0:1],
+            )
+
+        def interleave_rows(h, g):
+            hb[h, g] = sb("hb", [P, W, 4], BF16, bufs=2)
+            nc.vector.tensor_copy(
+                out=hb[h, g][:].rearrange("p (c i) t -> p c t i", i=4),
+                in_=hrows[h, g][:].rearrange("p t (c i) -> p c t i", i=4),
+            )
+
+        def quantise_h(h, g, parts=(0, 1)):
+            if 0 in parts:
+                hcodes[h, g] = sb("hcodes", [P, W], I32, bufs=8)
+                hscales[h, g] = sb("hscales", [P, W], U8, bufs=8)
+            cols = slice(256 * parts[0], 256 * (parts[-1] + 1))
             nc.vector.quantize_mx(
-                out=hcodes[h, g][:].bitcast(FP8X4), scales=hscales[h, g][:],
-                in_=hb[h, g][:].rearrange("p m t -> p (m t)"),
+                out=hcodes[h, g][:, cols].bitcast(FP8X4), scales=hscales[h, g][:, cols],
+                in_=hb[h, g][:, cols, :].rearrange("p m t -> p (m t)"),
             )
 
         chunks = [(0, 256), (256, 256), (512, 256), (768, 128), (896, 128)]
-        logd, yt, yb = {}, {}, {}
-
-        ring = tbank + zbank
-        taken = []
-        dbank, ybank = {}, {}
-
-        def next_bank():
-            taken.append(ring[len(taken) % len(ring)])
-            return taken[-1]
-
-        def dplace(c, t):
-            return dbank[c, t][:, 0:chunks[c][1]]
+        dbank, ybank, logd, yt, yb = {}, {}, {}, {}, {}
 
         def totals(c, t):
             m0, width = chunks[c]
             h, cols = m0 // W, slice(m0 % W, m0 % W + width)
-            dbank[c, t] = next_bank()
+            dbank[c, t] = next_bank()[:, 0:width]
             for g in range(GROUPS):
                 nc.tensor.matmul_mx(
-                    out=dplace(c, t),
+                    out=dbank[c, t],
                     lhsT=tw[:, g, t * P:(t + 1) * P].bitcast(FP8X4), lhsT_scale=ts[4 * g:P, t * P:(t + 1) * P],
                     rhs=hcodes[h, g][:, cols].bitcast(FP8X4), rhs_scale=hscales[h, g][:, cols],
                     start=(g == 0), stop=(g == GROUPS - 1),
@@ -174,22 +189,22 @@ def tile_near_duplicate_slice_density_k6_kernel(
         def log_density(c, t):
             width = chunks[c][1]
             if t == 0:
-                logd[c] = sb(f"logd{c}", [P, 4, width], F32)
+                logd[c] = sb("logd", [P, 4, width], F32, bufs=3)
             nc.scalar.activation(
-                out=logd[c][:, t, :], in_=dplace(c, t), func=ACT.Ln, bias=prior32[:, t:t + 1], scale=1.0,
+                out=logd[c][:, t, :], in_=dbank[c, t], func=ACT.Ln, bias=prior32[:, t:t + 1], scale=1.0,
             )
 
         def apply_gain(c, t):
             width = chunks[c][1]
             if t == 0:
-                yt[c] = sb(f"yt{c}", [P, 4, width], F32)
+                yt[c] = sb("yt", [P, 4, width], F32, bufs=3)
             nc.vector.tensor_scalar(
                 out=yt[c][:, t, :], in0=logd[c][:, t, :], scalar1=gain32[:, t:t + 1], scalar2=None, op0=ALU.mult,
             )
 
         def round_y(c):
             width = chunks[c][1]
-            yb[c] = sb(f"yb{c}", [P, width, 4], BF16)
+            yb[c] = sb("yb", [P, width, 4], BF16, bufs=2)
             nc.vector.tensor_copy(
                 out=yb[c][:].rearrange("p (c i) t -> p c t i", i=2),
                 in_=yt[c][:].rearrange("p t (c i) -> p c t i", i=2),
@@ -212,7 +227,7 @@ def tile_near_duplicate_slice_density_k6_kernel(
                 nc.tensor.transpose(ybank[c, j][:, t * P:(t + 1) * P], yt[c][:, t, j * P:(j + 1) * P], ident[:])
 
         def store_y(c, j, engine):
-            y = sb("y", [P, F], F32, bufs=6)
+            y = sb("y", [P, F], F32, bufs=5)
             out = y[:].rearrange("p (q t) -> p q t", t=4)
             in_ = ybank[c, j][:].rearrange("p (t q) -> p q t", t=4)
             if engine == "s":
@@ -247,137 +262,21 @@ def tile_near_duplicate_slice_density_k6_kernel(
         z0, z1, z2 = ("x", 1, 0), ("x", 1, 1), ("x", 1, 2)
         b0, b1, b2, b3 = (("bank", g) for g in range(GROUPS))
 
-        nc.gpsimd.memset(warm[:], 0.0)
-        make_identity(nc, ident[:])
-        load(x0, 2)
-        for a in range(2):
-            nc.scalar.dma_start(
-                out=bs_raw[a:P:2, :].bitcast(I32),
-                in_=bankb_scales[a].rearrange("q (g n) -> (q g) n", g=GROUPS).bitcast(I32),
-            )
-        nc.scalar.activation(out=first[:], in_=warm[:, 0:1], func=ACT.Sigmoid)
-        load(b0, 2)
-        load(x1, 2)
-        load(x2, 2)
-        load_bankb_words(0)
-        nc.vector.memset(bs[:].rearrange("p g a n -> p (g a n)").bitcast(I32), 0)
-        nc.vector.memset(ts_raw[:].bitcast(I32), 0)
-        nc.vector.tensor_copy(
-            out=bs_ordered[:].rearrange("p (t q) -> p t q", t=4), in_=bs_raw[:].rearrange("p (q t) -> p t q", t=4),
-        )
-        load(b1)
-        for q in (0, 2, 1, 3):
-            nc.sync.dma_start(
-                out=bs[32 * q:32 * q + 4].rearrange("p g a n -> p (g a) n").bitcast(I32),
-                in_=bs_ordered[32 * q:32 * (q + 1), :].bitcast(I32),
-            )
-        nc.sync.dma_start(out=tau_raw[:], in_=tau.rearrange("(g p t) -> p g t", p=P, t=4))
-        load_bankb_words(1)
-        load(b2)
-        nc.sync.dma_start(out=w_raw[:], in_=weight.rearrange("(g p t) -> p g t", p=P, t=4))
-        load_bankb_words(2)
-        load(b3)
-        load(z0)
-        load_bankb_words(3)
-        load(z1)
-        load(z2)
-        nc.sync.dma_start(out=tw_raw[:], in_=table_words.rearrange("g p f b -> p g (f b)").bitcast(I32))
-        for q in range(4):
-            nc.sync.dma_start(
-                out=ts_raw[32 * q:32 * q + 16, :].bitcast(I32), in_=table_scales[:, 4 * q:4 * q + 4, :].bitcast(I32),
-            )
-        nc.sync.dma_start(out=prior_raw[:], in_=prior.rearrange("(p t) -> p t", t=4))
-        nc.sync.dma_start(out=gain_raw[:], in_=gain.rearrange("(p t) -> p t", t=4))
-
         def keep_warm(width):
-            nc.tensor.matmul(zbank[0][:, 0:width], lhsT=warm[:, 0:P], rhs=warm[:, 0:width], start=True, stop=True)
+            nc.tensor.matmul(ring[7][:, 0:width], lhsT=warm[:, 0:P], rhs=warm[:, 0:width], start=True, stop=True)
 
-        for i in range(WARMUP):
-            keep_warm(W)
-
-        def step(h, g):
-            for t in range(4):
+        def step(h, g, ts_=range(4), rows=None):
+            for t in ts_:
                 for a in range(3):
                     gram(h, g, t, a)
                 sigmoid(h, g, t)
+                if rows is not None:
+                    weigh_rows(*rows, t)
 
-        turn(x0, 0)
-        pair_up(x0, 0, "sv")
-        keep_warm(256)
-        turn(b0, 2)
-        pair_up(b0, 2, "ss")
-        quantise(x0)
-        keep_warm(256)
-        turn(x1, 0)
-        pair_up(x1, 0, "ss")
-        quantise(b0)
-        keep_warm(256)
-        turn(x2, 2)
-        pair_up(x2, 2, "ss")
-        quantise(x1)
-        order_bankb_words(0, [0])
-        for t in range(4):
-            gram(0, 0, t, 0)
-        quantise(x2)
-        order_bankb_words(0, [1])
-        nc.vector.tensor_scalar(
-            out=neg_tau[:], in0=tau_raw[:].rearrange("p g t -> p (g t)"), scalar1=-1.0, scalar2=None, op0=ALU.mult,
-        )
-        turn(b1, 0)
-        pair_up(b1, 0, "ss")
-        for t in range(4):
-            gram(0, 0, t, 1)
-            gram(0, 0, t, 2)
-            sigmoid(0, 0, t)
-        order_bankb_words(1)
-        quantise(b1)
-        turn(b2, 2)
-        pair_up(b2, 2, "ss")
-        for i in range(2):
-            nc.vector.tensor_copy(out=w2[:, :, i], in_=w_raw[:].rearrange("p g t -> p (g t)"))
-        order_bankb_words(2)
-        weigh(0, 0, 0)
-        quantise(b2)
-        weigh(0, 0, 1)
-        step(0, 1)
-        turn(b3, 0)
-        pair_up(b3, 0, "ss")
-        turn(z0, 2)
-        pair_up(z0, 2, "ss")
-        order_bankb_words(3)
-        quantise_h(0, 0)
-        weigh(0, 1, 0)
-        quantise(b3)
-        quantise(z0)
-        weigh(0, 1, 1)
-        step(0, 2)
-        turn(z1, 0)
-        pair_up(z1, 0, "ss")
-        turn(z2, 2)
-        pair_up(z2, 2, "ss")
-        nc.vector.tensor_copy(
-            out=tw[:].rearrange("p g (t q) -> p g q t", t=4), in_=tw_raw[:].rearrange("p g (q t) -> p g q t", t=4),
-        )
-        quantise_h(0, 1)
-        nc.vector.tensor_copy(
-            out=ts[:].rearrange("p (t q) -> p t q", t=4), in_=ts_raw[:].rearrange("p (q t) -> p t q", t=4),
-        )
-        weigh(0, 2, 0)
-        quantise(z1)
-        quantise(z2)
-        weigh(0, 2, 1)
-        step(0, 3)
-        nc.vector.tensor_copy(out=prior32[:], in_=prior_raw[:])
-        nc.vector.tensor_copy(out=gain32[:], in_=gain_raw[:])
-        order = [(0, 2), (0, 3), (1, 0), (1, 1), (1, 2), (1, 3)]
-        for i in range(1, 6):
-            if i < 5:
-                step(*order[i + 1])
-            weigh(*order[i], 0)
-            quantise_h(*order[i - 1])
-            weigh(*order[i], 1)
-
-        nc.scalar.activation(out=first[:], in_=prior32[:, 0:1], func=ACT.Ln)
+        def turn_both(u, engines="ss"):
+            for half in range(2):
+                turn(u, half)
+                pair_up(u, half, engines[half])
 
         def slices(c, ts_):
             for t in ts_:
@@ -388,26 +287,160 @@ def tile_near_duplicate_slice_density_k6_kernel(
             for t in ts_:
                 apply_gain(c, t)
 
+        nc.gpsimd.memset(warm[:], 0.0)
+        make_identity(nc, ident[:])
+        load("xa", 0, 2)
+        for a in range(2):
+            nc.scalar.dma_start(
+                out=bs_raw[a:P:2, :].bitcast(I32),
+                in_=bankb_scales[a].rearrange("q (g n) -> (q g) n", g=GROUPS).bitcast(I32),
+            )
+        nc.scalar.activation(out=first[:], in_=warm[:, 0:1], func=ACT.Sigmoid)
+        load("bank", 0, 2)
+        load("xb", 0, 4)
+        nc.vector.memset(bs[:].rearrange("p g a n -> p (g a n)").bitcast(I32), 0)
+        nc.vector.memset(ts_raw[:].bitcast(I32), 0)
+        nc.vector.tensor_copy(
+            out=bs_ordered[:].rearrange("p (t q) -> p t q", t=4), in_=bs_raw[:].rearrange("p (q t) -> p t q", t=4),
+        )
+        load("bank", 1)
+        load_bankb_words(0, 0)
+        load("bank", 2)
+        for q in (0, 2, 1, 3):
+            nc.sync.dma_start(
+                out=bs[32 * q:32 * q + 4].rearrange("p g a n -> p (g a) n").bitcast(I32),
+                in_=bs_ordered[32 * q:32 * (q + 1), :].bitcast(I32),
+            )
+        load_bankb_words(1, 0)
+        nc.sync.dma_start(out=tau_raw[:], in_=tau.rearrange("(g p t) -> p g t", p=P, t=4))
+        nc.sync.dma_start(out=w_raw[:], in_=weight.rearrange("(g p t) -> p g t", p=P, t=4))
+        load_bankb_words(0, 1)
+        load_bankb_words(1, 1)
+        load("bank", 3)
+        load("xa", 1)
+        load("xb", 1)
+        nc.sync.dma_start(out=tw_raw[:], in_=table_words.rearrange("g p f b -> p g (f b)").bitcast(I32))
+        for q in range(4):
+            nc.sync.dma_start(
+                out=ts_raw[32 * q:32 * q + 16, :].bitcast(I32), in_=table_scales[:, 4 * q:4 * q + 4, :].bitcast(I32),
+            )
+        nc.sync.dma_start(out=prior_raw[:], in_=prior.rearrange("(p t) -> p t", t=4))
+        nc.sync.dma_start(out=gain_raw[:], in_=gain.rearrange("(p t) -> p t", t=4))
+        for i in range(WARMUP):
+            keep_warm(W)
+
+        turn_both(x0, "sv")
+        keep_warm(256)
+        turn_both(b0)
+        quantise(x0)
+        keep_warm(256)
+        for half in range(2):
+            for jj in range(2):
+                for u in (x1, x2):
+                    turn(u, half, [jj])
+            for u in (x1, x2):
+                pair_up(u, half)
+            if half == 0:
+                keep_warm(256)
+                quantise(b0)
+        quantise(x1)
+        quantise(x2)
+        for t in range(4):
+            gram(0, 0, t, 0)
+        turn_both(b1)
+        turn_both(b2)
+        order_bankb_words(0, 0)
+        order_bankb_words(1, 0)
+        quantise(b1)
+        order_bankb_words(0, 1)
+        nc.vector.tensor_scalar(
+            out=neg_tau[:], in0=tau_raw[:].rearrange("p g t -> p (g t)"), scalar1=-1.0, scalar2=None, op0=ALU.mult,
+        )
+        taken.extend(ring[:4])
+        for t in range(4):
+            gram(0, 0, t, 1)
+        for t in range(4):
+            gram(0, 0, t, 2)
+            sigmoid(0, 0, t)
+        order_bankb_words(1, 1)
+        quantise(b2)
+        for i in range(2):
+            nc.vector.tensor_copy(out=w2[:, :, i], in_=w_raw[:].rearrange("p g t -> p (g t)"))
+        order_bankb_words(2, 0)
+        order_bankb_words(2, 1)
+        step(0, 1)
+        split_words(b3)
+        weigh(0, 0, 0)
+        split_words(z0)
+        weigh(0, 0, 1)
+        split_words(z1)
+        split_words(z2)
+        quantise_h(0, 0)
+        step(0, 2, [0, 1])
+        for u in (b3, z0, z1, z2):
+            turn_both(u)
+        order_bankb_words(3, 0)
+        order_bankb_words(3, 1)
+        quantise(b3)
+        weigh(0, 1, 0)
+        quantise(z0)
+        weigh(0, 1, 1)
+        quantise(z1)
+        quantise(z2)
+        quantise_h(0, 1)
+        step(0, 2, [2, 3])
+        step(0, 3)
+        weigh(0, 2, 0)
+        weigh(0, 2, 1)
+        step(1, 0)
+        weigh(0, 3, 0)
+        quantise_h(0, 2)
+        weigh(0, 3, 1)
+        step(1, 1)
+        weigh(1, 0, 0)
+        quantise_h(0, 3)
+        weigh(1, 0, 1)
+        nc.vector.tensor_copy(
+            out=tw[:].rearrange("p g (t q) -> p g q t", t=4), in_=tw_raw[:].rearrange("p g (q t) -> p g q t", t=4),
+        )
+        step(1, 2)
+        weigh(1, 1, 0)
+        quantise_h(1, 0)
+        weigh(1, 1, 1)
+        nc.vector.tensor_copy(
+            out=ts[:].rearrange("p (t q) -> p t q", t=4), in_=ts_raw[:].rearrange("p (q t) -> p t q", t=4),
+        )
+        nc.vector.tensor_copy(out=prior32[:], in_=prior_raw[:])
+        nc.vector.tensor_copy(out=gain32[:], in_=gain_raw[:])
+        step(1, 3)
+        weigh(1, 2, 0)
+        quantise_h(1, 1)
+        weigh(1, 2, 1)
+        weigh(1, 3, 0)
+        quantise_h(1, 2)
+        quantise_h(1, 3, [0])
+
+        nc.scalar.activation(out=first[:], in_=prior32[:, 0:1], func=ACT.Ln)
+
         slices(0, range(4))
         slices(1, range(4))
-        gains(0, [0])
-        quantise_h(1, 3)
-        gains(0, [1, 2, 3])
+        gains(0, range(4))
+        weigh(1, 3, 1)
         slices(2, [0, 1])
         gains(1, range(4))
-        round_y(0)
-        for j in range(2):
-            turn_y(0, j)
+        quantise_h(1, 3, [1])
+        for c in range(2):
+            for j in range(2):
+                turn_y(c, j)
         store_y(0, 0, "s")
-        gains(2, [0])
-        quantise_y(0)
-        store_y(0, 1, "v")
-        slices(2, [2, 3])
-        for j in range(2):
-            turn_y(1, j)
-            store_y(1, j, "s")
+        store_y(0, 1, "s")
+        store_y(1, 0, "s")
+        round_y(0)
         round_y(1)
-        gains(2, [1, 2, 3])
+        quantise_y(0)
+        slices(2, [2, 3])
+        store_y(1, 1, "s")
+        gains(2, range(4))
         quantise_y(1)
         slices(3, range(4))
         round_y(2)
@@ -428,8 +461,8 @@ def tile_near_duplicate_slice_density_k6_kernel(
         turn_y(4, 0)
         round_y(4)
         quantise_y(4)
+        store_y(4, 0, "s")
         for q in range(4):
-            nc.sync.dma_start(
+            nc.scalar.dma_start(
                 out=out_2[0, 4 * q:4 * q + 4, :].bitcast(I32), in_=yscales[32 * q:32 * q + 4, :].bitcast(I32),
             )
-        store_y(4, 0, "s")

@@ -77,7 +77,7 @@ def tile_near_duplicate_slice_density_k6_kernel(
 
         def pair_up(u, half, engine="s"):
             if half == 0:
-                grouped[u] = sb("grouped", [P, 2 * W], F32, bufs=4)
+                grouped[u] = sb("grouped", [P, 2 * W], F32, bufs=3)
             if u[0] == "bank":
                 out = grouped[u][:].rearrange("p (h j r e) -> p h j r e", h=2, j=2, e=2)[:, half]
                 in_ = turned[u, half][:].rearrange("p (j e r) -> p j r e", j=2, e=2)
@@ -136,7 +136,7 @@ def tile_near_duplicate_slice_density_k6_kernel(
 
         def weigh(h, g, part):
             if part == 0:
-                hb[h, g] = sb("hb", [P, W, 4], BF16, bufs=2)
+                hb[h, g] = sb("hb", [P, W, 4], BF16, bufs=3)
             cols = slice(part * 256, (part + 1) * 256)
             nc.vector.tensor_tensor(
                 out=hb[h, g][:, cols, :].rearrange("p (c i) t -> p c t i", i=2),
@@ -155,7 +155,7 @@ def tile_near_duplicate_slice_density_k6_kernel(
             )
 
         def interleave_rows(h, g):
-            hb[h, g] = sb("hb", [P, W, 4], BF16, bufs=2)
+            hb[h, g] = sb("hb", [P, W, 4], BF16, bufs=3)
             nc.vector.tensor_copy(
                 out=hb[h, g][:].rearrange("p (c i) t -> p c t i", i=4),
                 in_=hrows[h, g][:].rearrange("p t (c i) -> p c t i", i=4),
@@ -227,7 +227,7 @@ def tile_near_duplicate_slice_density_k6_kernel(
                 nc.tensor.transpose(ybank[c, j][:, t * P:(t + 1) * P], yt[c][:, t, j * P:(j + 1) * P], ident[:])
 
         def store_y(c, j, engine):
-            y = sb("y", [P, F], F32, bufs=5)
+            y = sb("y", [P, F], F32, bufs=4)
             out = y[:].rearrange("p (q t) -> p q t", t=4)
             in_ = ybank[c, j][:].rearrange("p (t q) -> p q t", t=4)
             if engine == "s":
@@ -287,14 +287,23 @@ def tile_near_duplicate_slice_density_k6_kernel(
             for t in ts_:
                 apply_gain(c, t)
 
+        def spread(pair):
+            for q in (0, 2, 1, 3):
+                rows = slice(64 * pair + 16 * q, 64 * pair + 16 * (q + 1))
+                nc.sync.dma_start(
+                    out=bs[32 * q:32 * q + 4, 2 * pair:2 * pair + 2].rearrange("p g a n -> p (g a) n").bitcast(I32),
+                    in_=bs_ordered[rows, :].bitcast(I32),
+                )
+
         nc.gpsimd.memset(warm[:], 0.0)
         make_identity(nc, ident[:])
         load("xa", 0, 2)
-        for a in range(2):
-            nc.scalar.dma_start(
-                out=bs_raw[a:P:2, :].bitcast(I32),
-                in_=bankb_scales[a].rearrange("q (g n) -> (q g) n", g=GROUPS).bitcast(I32),
-            )
+        for pair in range(2):
+            for a in range(2):
+                nc.scalar.dma_start(
+                    out=bs_raw[64 * pair + a:64 * (pair + 1):2, :].bitcast(I32),
+                    in_=bankb_scales[a, :, 2 * W * pair:2 * W * (pair + 1)].rearrange("q (g n) -> q g n", g=2).bitcast(I32),
+                )
         nc.scalar.activation(out=first[:], in_=warm[:, 0:1], func=ACT.Sigmoid)
         load("bank", 0, 2)
         load("xb", 0, 4)
@@ -306,17 +315,14 @@ def tile_near_duplicate_slice_density_k6_kernel(
         load("bank", 1)
         load_bankb_words(0, 0)
         load("bank", 2)
-        for q in (0, 2, 1, 3):
-            nc.sync.dma_start(
-                out=bs[32 * q:32 * q + 4].rearrange("p g a n -> p (g a) n").bitcast(I32),
-                in_=bs_ordered[32 * q:32 * (q + 1), :].bitcast(I32),
-            )
+        spread(0)
         load_bankb_words(1, 0)
         nc.sync.dma_start(out=tau_raw[:], in_=tau.rearrange("(g p t) -> p g t", p=P, t=4))
         nc.sync.dma_start(out=w_raw[:], in_=weight.rearrange("(g p t) -> p g t", p=P, t=4))
         load_bankb_words(0, 1)
         load_bankb_words(1, 1)
         load("bank", 3)
+        spread(1)
         load("xa", 1)
         load("xb", 1)
         nc.sync.dma_start(out=tw_raw[:], in_=table_words.rearrange("g p f b -> p g (f b)").bitcast(I32))
@@ -351,8 +357,8 @@ def tile_near_duplicate_slice_density_k6_kernel(
         turn_both(b2)
         order_bankb_words(0, 0)
         order_bankb_words(1, 0)
-        quantise(b1)
         order_bankb_words(0, 1)
+        quantise(b1)
         nc.vector.tensor_scalar(
             out=neg_tau[:], in0=tau_raw[:].rearrange("p g t -> p (g t)"), scalar1=-1.0, scalar2=None, op0=ALU.mult,
         )
@@ -392,30 +398,29 @@ def tile_near_duplicate_slice_density_k6_kernel(
         step(0, 3)
         weigh(0, 2, 0)
         weigh(0, 2, 1)
-        step(1, 0)
-        weigh(0, 3, 0)
-        quantise_h(0, 2)
-        weigh(0, 3, 1)
-        step(1, 1)
-        weigh(1, 0, 0)
-        quantise_h(0, 3)
-        weigh(1, 0, 1)
+        step(1, 0, rows=(0, 3))
         nc.vector.tensor_copy(
             out=tw[:].rearrange("p g (t q) -> p g q t", t=4), in_=tw_raw[:].rearrange("p g (q t) -> p g q t", t=4),
         )
-        step(1, 2)
-        weigh(1, 1, 0)
-        quantise_h(1, 0)
-        weigh(1, 1, 1)
+        quantise_h(0, 2)
         nc.vector.tensor_copy(
             out=ts[:].rearrange("p (t q) -> p t q", t=4), in_=ts_raw[:].rearrange("p (q t) -> p t q", t=4),
         )
         nc.vector.tensor_copy(out=prior32[:], in_=prior_raw[:])
         nc.vector.tensor_copy(out=gain32[:], in_=gain_raw[:])
-        step(1, 3)
+        weigh(1, 0, 0)
+        weigh(1, 0, 1)
+        step(1, 1)
+        interleave_rows(0, 3)
+        quantise_h(1, 0)
+        weigh(1, 1, 0)
+        quantise_h(0, 3)
+        weigh(1, 1, 1)
+        step(1, 2)
         weigh(1, 2, 0)
         quantise_h(1, 1)
         weigh(1, 2, 1)
+        step(1, 3)
         weigh(1, 3, 0)
         quantise_h(1, 2)
         quantise_h(1, 3, [0])

@@ -58,12 +58,15 @@ def tile_near_duplicate_slice_density_k6_kernel(
             else:
                 raw["bank", i] = tile[:]
 
-        def split_words(u):
+        def split_words(u, engine="v"):
             split[u] = sb("split", [P, 4, 2, P], F32, bufs=4)
-            nc.vector.tensor_copy(
-                out=split[u][:].rearrange("p j e q -> p j q e"),
-                in_=raw[u].bitcast(F32).rearrange("p j (q e) -> p j q e", e=2),
-            )
+            words = raw[u].bitcast(F32)
+            if engine == "s":
+                nc.scalar.copy(out=split[u][:], in_=words.rearrange("p j (q e) -> p j e q", e=2))
+            else:
+                nc.vector.tensor_copy(
+                    out=split[u][:].rearrange("p j e q -> p j q e"), in_=words.rearrange("p j (q e) -> p j q e", e=2),
+                )
 
         def turn(u, half, jjs=(0, 1)):
             if 0 in jjs:
@@ -375,9 +378,9 @@ def tile_near_duplicate_slice_density_k6_kernel(
         order_bankb_words(2, 0)
         order_bankb_words(2, 1)
         step(0, 1)
+        split_words(z0, "s")
         split_words(b3)
         weigh(0, 0, 0)
-        split_words(z0)
         weigh(0, 0, 1)
         split_words(z1)
         split_words(z2)
@@ -386,17 +389,17 @@ def tile_near_duplicate_slice_density_k6_kernel(
         for u in (b3, z0, z1, z2):
             turn_both(u)
         order_bankb_words(3, 0)
-        order_bankb_words(3, 1)
         quantise(b3)
-        weigh(0, 1, 0)
+        order_bankb_words(3, 1)
         quantise(z0)
-        weigh(0, 1, 1)
+        weigh(0, 1, 0)
         quantise(z1)
         quantise(z2)
-        quantise_h(0, 1)
+        weigh(0, 1, 1)
         step(0, 2, [2, 3])
         step(0, 3)
         weigh(0, 2, 0)
+        quantise_h(0, 1)
         weigh(0, 2, 1)
         step(1, 0, rows=(0, 3))
         nc.vector.tensor_copy(
@@ -430,10 +433,9 @@ def tile_near_duplicate_slice_density_k6_kernel(
         slices(0, range(4))
         slices(1, range(4))
         gains(0, range(4))
-        weigh(1, 3, 1)
         slices(2, [0, 1])
         gains(1, range(4))
-        quantise_h(1, 3, [1])
+        weigh(1, 3, 1)
         for c in range(2):
             for j in range(2):
                 turn_y(c, j)
@@ -441,6 +443,7 @@ def tile_near_duplicate_slice_density_k6_kernel(
         store_y(0, 1, "s")
         store_y(1, 0, "s")
         round_y(0)
+        quantise_h(1, 3, [1])
         round_y(1)
         quantise_y(0)
         slices(2, [2, 3])

from contextlib import ExitStack

import concourse.mybir as mybir
from concourse.masks import make_identity

M, N, KA, KB, F = 1024, 2048, 512, 1024, 512
FLOPS = 2 * M * N * (KA + KB) + 2 * M * N * F

F32 = mybir.dt.float32
BF16 = mybir.dt.bfloat16
I32 = mybir.dt.int32
U8 = mybir.dt.uint8
FP8X4 = mybir.dt.float8_e4m3fn_x4
FP4X4 = mybir.dt.float4_e2m1fn_x4
ACT = mybir.ActivationFunctionType
ALU = mybir.AluOpType

P = 128
W = 512
GROUPS = N // W
WARMUP = 4


def tile_near_duplicate_slice_density_k6_kernel(
    tc, batch_a, batch_b, bank_a, bankb_words, bankb_scales, tau, weight, table_words, table_scales,
    prior, gain, out_0, out_1, out_2,
):
    nc = tc.nc
    with ExitStack() as ctx:
        keep = ctx.enter_context(tc.tile_pool(name="keep", bufs=1))
        psum = ctx.enter_context(tc.psum_pool(name="psum", bufs=1))
        ctx.enter_context(tc.manual_schedule())

        def sb(name, shape, dtype, bufs=1):
            return keep.tile(shape, dtype, name=name, tag=name, bufs=bufs, align_bytes=64)

        ring = [psum.tile([P, W], F32, name=f"bank{i}") for i in range(8)]
        taken = []

        def next_bank():
            taken.append(ring[len(taken) % len(ring)])
            return taken[-1]

        raw, split, grouped, codes, scales, turned = {}, {}, {}, {}, {}, {}

        def load(name, i, pieces=1):
            source = {"xa": batch_a, "xb": batch_b, "bank": bank_a}[name]
            k = source.shape[1]
            tile = sb("raw_wide", [P, 4, k], BF16, bufs=2) if name == "xb" else sb("raw", [P, 4, k], BF16, bufs=4)
            rows = source[i * W:(i + 1) * W, :].rearrange("(p j) k -> p j k", j=4)
            for piece in range(pieces):
                js = slice(piece * 4 // pieces, (piece + 1) * 4 // pieces)
                nc.sync.dma_start(out=tile[:, js, :], in_=rows[:, js, :])
            if name == "xb":
                raw["x", i, 1], raw["x", i, 2] = tile[:, :, 0:W], tile[:, :, W:2 * W]
            elif name == "xa":
                raw["x", i, 0] = tile[:]
            else:
                raw["bank", i] = tile[:]

        def split_words(u, engine="v"):
            split[u] = sb("split", [P, 4, 2, P], F32, bufs=4)
            words = raw[u].bitcast(F32)
            if engine == "s":
                nc.scalar.copy(out=split[u][:], in_=words.rearrange("p j (q e) -> p j e q", e=2))
            else:
                nc.vector.tensor_copy(
                    out=split[u][:].rearrange("p j e q -> p j q e"), in_=words.rearrange("p j (q e) -> p j q e", e=2),
                )

        def turn(u, half, jjs=(0, 1)):
            if 0 in jjs:
                turned[u, half] = next_bank()
            for jj in jjs:
                j = 2 * half + jj
                for e in range(2):
                    in_ = split[u][:, j, e, :] if u in split else raw[u][:, j, :].bitcast(F32)[:, e:256:2]
                    col = (2 * jj + e) * P
                    nc.tensor.transpose(turned[u, half][:, col:col + P], in_, ident[:])

        def pair_up(u, half, engine="s"):
            if half == 0:
                grouped[u] = sb("grouped", [P, 2 * W], F32, bufs=3)
            if u[0] == "bank":
                out = grouped[u][:].rearrange("p (h j r e) -> p h j r e", h=2, j=2, e=2)[:, half]
                in_ = turned[u, half][:].rearrange("p (j e r) -> p j r e", j=2, e=2)
            else:
                out = grouped[u][:].rearrange("p (r h j e) -> p h r j e", h=2, j=2, e=2)[:, half]
                in_ = turned[u, half][:].rearrange("p (j e r) -> p r j e", j=2, e=2)
            if engine == "s":
                nc.scalar.copy(out=out, in_=in_)
            else:
                nc.vector.tensor_copy(out=out, in_=in_)

        def quantise(u):
            codes[u] = sb("codes", [P, W], I32, bufs=10)
            scales[u] = sb("scales", [P, W], U8, bufs=10)
            nc.vector.quantize_mx(out=codes[u][:].bitcast(FP8X4), scales=scales[u][:], in_=grouped[u][:].bitcast(BF16))

        bw_raw, bw = {}, {}

        def load_bankb_words(a, pair):
            tile = sb("bw_raw", [P, 2, 2 * W], U8, bufs=4)
            in_ = bankb_words[a, :, 4 * W * pair:4 * W * (pair + 1)]
            nc.sync.dma_start(out=tile[:].rearrange("p g b -> p (g b)").bitcast(I32), in_=in_.bitcast(I32))
            bw_raw[2 * pair, a], bw_raw[2 * pair + 1, a] = tile[:, 0, :], tile[:, 1, :]

        def order_bankb_words(g, a):
            bw[g, a] = sb("bw", [P, 2 * W], U8, bufs=8)
            nc.vector.tensor_copy(
                out=bw[g, a][:].rearrange("p (t q b) -> p t q b", t=4, b=2),
                in_=bw_raw[g, a].rearrange("p (q t b) -> p t q b", t=4, b=2),
            )

        zbank, sig, hb, hcodes, hscales = {}, {}, {}, {}, {}

        def gram(h, g, t, a):
            cols = slice(t * P, (t + 1) * P)
            if a == 0:
                zbank[h, g, t] = next_bank()
                lhsT = codes["bank", g][:, cols].bitcast(FP8X4)
                lhsT_scale = scales["bank", g][:, cols]
            else:
                lhsT = bw[g, a - 1][:, 2 * t * P:2 * (t + 1) * P].bitcast(FP4X4)
                lhsT_scale = bs[:, g, a - 1, cols]
            nc.tensor.matmul_mx(
                out=zbank[h, g, t][:], lhsT=lhsT, lhsT_scale=lhsT_scale,
                rhs=codes["x", h, a][:].bitcast(FP8X4), rhs_scale=scales["x", h, a][:],
                start=(a == 0), stop=(a == 2),
            )

        def sigmoid(h, g, t):
            if t == 0:
                sig[h, g] = sb("sig", [P, 4, W], F32, bufs=4)
            nc.scalar.activation(
                out=sig[h, g][:, t, :], in_=zbank[h, g, t][:], func=ACT.Sigmoid,
                bias=neg_tau[:, 4 * g + t:4 * g + t + 1], scale=1.0,
            )

        def weigh(h, g, part):
            if part == 0:
                hb[h, g] = sb("hb", [P, W, 4], BF16, bufs=3)
            cols = slice(part * 256, (part + 1) * 256)
            nc.vector.tensor_tensor(
                out=hb[h, g][:, cols, :].rearrange("p (c i) t -> p c t i", i=2),
                in0=sig[h, g][:, :, cols].rearrange("p t (c i) -> p c t i", i=2),
                in1=w2[:, 4 * g:4 * g + 4, :].unsqueeze(1).to_broadcast([P, 128, 4, 2]),
                op=ALU.mult,
            )

        hrows = {}

        def weigh_rows(h, g, t):
            if t == 0:
                hrows[h, g] = sb("hrows", [P, 4, W], BF16, bufs=1)
            nc.scalar.activation(
                out=hrows[h, g][:, t, :], in_=sig[h, g][:, t, :], func=ACT.Copy, scale=w2[:, 4 * g + t, 0:1],
            )

        def interleave_rows(h, g):
            hb[h, g] = sb("hb", [P, W, 4], BF16, bufs=3)
            nc.vector.tensor_copy(
                out=hb[h, g][:].rearrange("p (c i) t -> p c t i", i=4),
                in_=hrows[h, g][:].rearrange("p t (c i) -> p c t i", i=4),
            )

        def quantise_h(h, g, parts=(0, 1)):
            if 0 in parts:
                hcodes[h, g] = sb("hcodes", [P, W], I32, bufs=8)
                hscales[h, g] = sb("hscales", [P, W], U8, bufs=8)
            cols = slice(256 * parts[0], 256 * (parts[-1] + 1))
            nc.vector.quantize_mx(
                out=hcodes[h, g][:, cols].bitcast(FP8X4), scales=hscales[h, g][:, cols],
                in_=hb[h, g][:, cols, :].rearrange("p m t -> p (m t)"),
            )

        chunks = [(0, 256), (256, 256), (512, 256), (768, 128), (896, 128)]
        dbank, ybank, logd, yt, yb = {}, {}, {}, {}, {}

        def totals(c, t):
            m0, width = chunks[c]
            h, cols = m0 // W, slice(m0 % W, m0 % W + width)
            dbank[c, t] = next_bank()[:, 0:width]
            for g in range(GROUPS):
                nc.tensor.matmul_mx(
                    out=dbank[c, t],
                    lhsT=tw[:, g, t * P:(t + 1) * P].bitcast(FP8X4), lhsT_scale=ts[4 * g:P, t * P:(t + 1) * P],
                    rhs=hcodes[h, g][:, cols].bitcast(FP8X4), rhs_scale=hscales[h, g][:, cols],
                    start=(g == 0), stop=(g == GROUPS - 1),
                )

        def log_density(c, t):
            width = chunks[c][1]
            if t == 0:
                logd[c] = sb("logd", [P, 4, width], F32, bufs=3)
            nc.scalar.activation(
                out=logd[c][:, t, :], in_=dbank[c, t], func=ACT.Ln, bias=prior32[:, t:t + 1], scale=1.0,
            )

        def apply_gain(c, t):
            width = chunks[c][1]
            if t == 0:
                yt[c] = sb("yt", [P, 4, width], F32, bufs=3)
            nc.vector.tensor_scalar(
                out=yt[c][:, t, :], in0=logd[c][:, t, :], scalar1=gain32[:, t:t + 1], scalar2=None, op0=ALU.mult,
            )

        def round_y(c):
            width = chunks[c][1]
            yb[c] = sb("yb", [P, width, 4], BF16, bufs=2)
            nc.vector.tensor_copy(
                out=yb[c][:].rearrange("p (c i) t -> p c t i", i=2),
                in_=yt[c][:].rearrange("p t (c i) -> p c t i", i=2),
            )

        def quantise_y(c):
            m0, width = chunks[c]
            nc.vector.quantize_mx(
                out=ycodes[:, m0:m0 + width].bitcast(FP8X4), scales=yscales[:, m0:m0 + width],
                in_=yb[c][:].rearrange("p m t -> p (m t)"),
            )
            nc.sync.dma_start(
                out=out_1[0].rearrange("p m t -> p (m t)").bitcast(I32)[:, m0:m0 + width],
                in_=ycodes[:, m0:m0 + width],
            )

        def turn_y(c, j):
            ybank[c, j] = next_bank()
            for t in range(4):
                nc.tensor.transpose(ybank[c, j][:, t * P:(t + 1) * P], yt[c][:, t, j * P:(j + 1) * P], ident[:])

        def store_y(c, j, engine):
            y = sb("y", [P, F], F32, bufs=4)
            out = y[:].rearrange("p (q t) -> p q t", t=4)
            in_ = ybank[c, j][:].rearrange("p (t q) -> p q t", t=4)
            if engine == "s":
                nc.scalar.copy(out=out, in_=in_)
            else:
                nc.vector.tensor_copy(out=out, in_=in_)
            m0 = chunks[c][0] + j * P
            nc.sync.dma_start(out=out_0[m0:m0 + P, :], in_=y[:])

        ident = sb("ident", [P, P], F32)
        warm = sb("warm", [P, W], BF16)
        bs_raw = sb("bs_raw", [P, W], U8)
        bs_ordered = sb("bs_ordered", [P, W], U8)
        bs = sb("bs", [P, GROUPS, 2, W], U8)
        ts_raw = sb("ts_raw", [P, W], U8)
        ts = sb("ts", [P, W], U8)
        tw_raw = sb("tw_raw", [P, GROUPS, F], I32)
        tw = sb("tw", [P, GROUPS, F], I32)
        tau_raw = sb("tau_raw", [P, GROUPS, 4], BF16)
        w_raw = sb("w_raw", [P, GROUPS, 4], BF16)
        prior_raw = sb("prior_raw", [P, 4], BF16)
        gain_raw = sb("gain_raw", [P, 4], BF16)
        neg_tau = sb("neg_tau", [P, 4 * GROUPS], F32)
        w2 = sb("w2", [P, 4 * GROUPS, 2], F32)
        prior32 = sb("prior32", [P, 4], F32)
        gain32 = sb("gain32", [P, 4], F32)
        ycodes = sb("ycodes", [P, M], I32)
        yscales = sb("yscales", [P, M], U8)
        first = sb("first", [P, 1], F32)

        x0, x1, x2 = ("x", 0, 0), ("x", 0, 1), ("x", 0, 2)
        z0, z1, z2 = ("x", 1, 0), ("x", 1, 1), ("x", 1, 2)
        b0, b1, b2, b3 = (("bank", g) for g in range(GROUPS))

        def keep_warm(width):
            nc.tensor.matmul(ring[7][:, 0:width], lhsT=warm[:, 0:P], rhs=warm[:, 0:width], start=True, stop=True)

        def step(h, g, ts_=range(4), rows=None):
            for t in ts_:
                for a in range(3):
                    gram(h, g, t, a)
                sigmoid(h, g, t)
                if rows is not None:
                    weigh_rows(*rows, t)

        def turn_both(u, engines="ss"):
            for half in range(2):
                turn(u, half)
                pair_up(u, half, engines[half])

        def slices(c, ts_):
            for t in ts_:
                totals(c, t)
                log_density(c, t)

        def gains(c, ts_):
            for t in ts_:
                apply_gain(c, t)

        def spread(pair):
            for q in (0, 2, 1, 3):
                rows = slice(64 * pair + 16 * q, 64 * pair + 16 * (q + 1))
                nc.sync.dma_start(
                    out=bs[32 * q:32 * q + 4, 2 * pair:2 * pair + 2].rearrange("p g a n -> p (g a) n").bitcast(I32),
                    in_=bs_ordered[rows, :].bitcast(I32),
                )

        nc.gpsimd.memset(warm[:], 0.0)
        make_identity(nc, ident[:])
        load("xa", 0, 2)
        for pair in range(2):
            for a in range(2):
                nc.scalar.dma_start(
                    out=bs_raw[64 * pair + a:64 * (pair + 1):2, :].bitcast(I32),
                    in_=bankb_scales[a, :, 2 * W * pair:2 * W * (pair + 1)].rearrange("q (g n) -> q g n", g=2).bitcast(I32),
                )
        nc.scalar.activation(out=first[:], in_=warm[:, 0:1], func=ACT.Sigmoid)
        load("bank", 0, 2)
        load("xb", 0, 4)
        nc.vector.memset(bs[:].rearrange("p g a n -> p (g a n)").bitcast(I32), 0)
        nc.vector.memset(ts_raw[:].bitcast(I32), 0)
        nc.vector.tensor_copy(
            out=bs_ordered[:].rearrange("p (t q) -> p t q", t=4), in_=bs_raw[:].rearrange("p (q t) -> p t q", t=4),
        )
        load("bank", 1)
        load_bankb_words(0, 0)
        load("bank", 2)
        spread(0)
        load_bankb_words(1, 0)
        nc.sync.dma_start(out=tau_raw[:], in_=tau.rearrange("(g p t) -> p g t", p=P, t=4))
        nc.sync.dma_start(out=w_raw[:], in_=weight.rearrange("(g p t) -> p g t", p=P, t=4))
        load_bankb_words(0, 1)
        load_bankb_words(1, 1)
        load("bank", 3)
        spread(1)
        load("xa", 1)
        load("xb", 1)
        nc.sync.dma_start(out=tw_raw[:], in_=table_words.rearrange("g p f b -> p g (f b)").bitcast(I32))
        for q in range(4):
            nc.sync.dma_start(
                out=ts_raw[32 * q:32 * q + 16, :].bitcast(I32), in_=table_scales[:, 4 * q:4 * q + 4, :].bitcast(I32),
            )
        nc.sync.dma_start(out=prior_raw[:], in_=prior.rearrange("(p t) -> p t", t=4))
        nc.sync.dma_start(out=gain_raw[:], in_=gain.rearrange("(p t) -> p t", t=4))
        for i in range(WARMUP):
            keep_warm(W)

        turn_both(x0, "sv")
        keep_warm(256)
        turn_both(b0)
        quantise(x0)
        keep_warm(256)
        for half in range(2):
            for jj in range(2):
                for u in (x1, x2):
                    turn(u, half, [jj])
            for u in (x1, x2):
                pair_up(u, half)
            if half == 0:
                keep_warm(256)
                quantise(b0)
        quantise(x1)
        quantise(x2)
        for t in range(4):
            gram(0, 0, t, 0)
        turn_both(b1)
        turn_both(b2)
        order_bankb_words(0, 0)
        order_bankb_words(1, 0)
        order_bankb_words(0, 1)
        quantise(b1)
        nc.vector.tensor_scalar(
            out=neg_tau[:], in0=tau_raw[:].rearrange("p g t -> p (g t)"), scalar1=-1.0, scalar2=None, op0=ALU.mult,
        )
        taken.extend(ring[:4])
        for t in range(4):
            gram(0, 0, t, 1)
        for t in range(4):
            gram(0, 0, t, 2)
            sigmoid(0, 0, t)
        order_bankb_words(1, 1)
        quantise(b2)
        for i in range(2):
            nc.vector.tensor_copy(out=w2[:, :, i], in_=w_raw[:].rearrange("p g t -> p (g t)"))
        order_bankb_words(2, 0)
        order_bankb_words(2, 1)
        step(0, 1)
        split_words(z0, "s")
        split_words(b3)
        weigh(0, 0, 0)
        weigh(0, 0, 1)
        split_words(z1)
        split_words(z2)
        quantise_h(0, 0)
        step(0, 2, [0, 1])
        for u in (b3, z0, z1, z2):
            turn_both(u)
        order_bankb_words(3, 0)
        quantise(b3)
        order_bankb_words(3, 1)
        quantise(z0)
        weigh(0, 1, 0)
        quantise(z1)
        quantise(z2)
        weigh(0, 1, 1)
        step(0, 2, [2, 3])
        step(0, 3)
        weigh(0, 2, 0)
        quantise_h(0, 1)
        weigh(0, 2, 1)
        step(1, 0, rows=(0, 3))
        nc.vector.tensor_copy(
            out=tw[:].rearrange("p g (t q) -> p g q t", t=4), in_=tw_raw[:].rearrange("p g (q t) -> p g q t", t=4),
        )
        quantise_h(0, 2)
        nc.vector.tensor_copy(
            out=ts[:].rearrange("p (t q) -> p t q", t=4), in_=ts_raw[:].rearrange("p (q t) -> p t q", t=4),
        )
        nc.vector.tensor_copy(out=prior32[:], in_=prior_raw[:])
        nc.vector.tensor_copy(out=gain32[:], in_=gain_raw[:])
        weigh(1, 0, 0)
        weigh(1, 0, 1)
        step(1, 1)
        interleave_rows(0, 3)
        quantise_h(1, 0)
        weigh(1, 1, 0)
        quantise_h(0, 3)
        weigh(1, 1, 1)
        step(1, 2)
        weigh(1, 2, 0)
        quantise_h(1, 1)
        weigh(1, 2, 1)
        step(1, 3)
        weigh(1, 3, 0)
        quantise_h(1, 2)
        quantise_h(1, 3, [0])

        nc.scalar.activation(out=first[:], in_=prior32[:, 0:1], func=ACT.Ln)

        slices(0, range(4))
        slices(1, range(4))
        gains(0, range(4))
        slices(2, [0, 1])
        gains(1, range(4))
        weigh(1, 3, 1)
        for c in range(2):
            for j in range(2):
                turn_y(c, j)
        store_y(0, 0, "s")
        store_y(0, 1, "s")
        store_y(1, 0, "s")
        round_y(0)
        quantise_h(1, 3, [1])
        round_y(1)
        quantise_y(0)
        slices(2, [2, 3])
        store_y(1, 1, "s")
        gains(2, range(4))
        quantise_y(1)
        slices(3, range(4))
        round_y(2)
        gains(3, [0, 1])
        quantise_y(2)
        gains(3, [2, 3])
        for j in range(2):
            turn_y(2, j)
        store_y(2, 0, "s")
        store_y(2, 1, "v")
        slices(4, range(4))
        round_y(3)
        gains(4, [0, 1])
        quantise_y(3)
        gains(4, [2, 3])
        turn_y(3, 0)
        store_y(3, 0, "s")
        turn_y(4, 0)
        round_y(4)
        quantise_y(4)
        store_y(4, 0, "s")
        for q in range(4):
            nc.scalar.dma_start(
                out=out_2[0, 4 * q:4 * q + 4, :].bitcast(I32), in_=yscales[32 * q:32 * q + 4, :].bitcast(I32),
            )
